import numpy as np, ml_dtypes
CORES = [14,30,46,62,78,94,110,126,134,150,166,182,198,214,230,246]
N = 16
def setup_inputs(rng):
    return {"x": rng.standard_normal((N, 128, 32), dtype=np.float32).astype(ml_dtypes.bfloat16)}
def reference(x):
    s = x.sum(axis=0, dtype=np.float64).astype(x.dtype)
    b = 32 // N
    return {"y": np.stack([s[:, r * b:(r + 1) * b] for r in range(N)])}

@@ -1,0 +1,87 @@
+from concourse.bass import DstId, RemoteDMATransfer
+
+N = 16
+K = 4
+R = 2
+G = N // R
+W = 32 // K
+SPLIT_FOLD = False
+
+SCRATCH = {
+    "d": ("dram", [K * 128, W], "bfloat16"),
+    "land": ("dram", [N * 128, W], "bfloat16"),
+    "s": ("dram", [K * 128, W], "bfloat16"),
+}
+SEMAPHORES = ["loaded", "arr", "got", "sent", "stored"]
+
+
+def _bits(first, n):
+    return ((1 << n) - 1) << first
+
+
+def _slot(t, i):
+    return t[i * 128:(i + 1) * 128, :]
+
+
+def _reducer(T, k, q):
+    return T.cores[q * G + k * (G // K)] + 1
+
+
+def _dst(topo, dst, src):
+    rid, pid = topo.addr(dst, src)
+    return DstId(rid=rid, pnc=pid)
+
+
+E1 = max(1, 8 // (K * R))
+E2 = max(1, 8 // G) if SPLIT_FOLD else 8
+
+
+def rank_program(g, core, T, topo):
+    rank = T.rank_of(core)
+    if rank is not None:
+        g.sync.dma_start(T.d[:], T.x[:]).then_inc(T.sem.loaded, 16)
+        g.wait_ge(T.sem.loaded, 16)
+        tr = []
+        if K * R <= 8:
+            for k in range(K):
+                for q in range(R):
+                    tr.append(RemoteDMATransfer(
+                        dst_ids=[_dst(topo, _reducer(T, k, q), core)], dma_engine_mask=_bits((k * R + q) * E1, E1),
+                        remote_sem=T.sem.arr, src=_slot(T.d, k), dst=_slot(T.land, rank)))
+            sent = 8
+        else:
+            e = 8 // K
+            for k in range(K):
+                tr.append(RemoteDMATransfer(
+                    dst_ids=[_dst(topo, _reducer(T, k, q), core) for q in range(R)], dma_engine_mask=_bits(k * e, e),
+                    remote_sem=T.sem.arr, srcs=[_slot(T.d, k)], dsts=[_slot(T.land, rank)] * R))
+            sent = 8
+        g.remote_dma_fused(tr, local_sem=T.sem.sent)
+        w0 = 2 * rank
+        g.sync.wait_ge(T.sem.got, K * E2)
+        g.sync.dma_start(T.y[:], T.s[w0 // W::K, w0 % W:w0 % W + 2]).then_inc(T.sem.stored, 16)
+        g.sync.wait_ge(T.sem.stored, 16)
+        g.wait_ge(T.sem.sent, sent)
+        return
+
+    for k in range(K):
+        for q in range(R):
+            if _reducer(T, k, q) != core:
+                continue
+            e1 = E1 if K * R <= 8 else 8 // K
+            g.wait_ge(T.sem.arr, N * e1)
+            srcs = [_slot(T.land, i) for i in range(N)]
+            dsts = [T.cores[q * G + j] for j in range(G)]
+            if SPLIT_FOLD:
+                per = max(1, G // 8)
+                tr = []
+                for j in range(0, G, per):
+                    tr.append(RemoteDMATransfer(
+                        dst_ids=[_dst(topo, c, core) for c in dsts[j:j + per]], dma_engine_mask=_bits((j // per) * E2, E2),
+                        remote_sem=T.sem.got, srcs=srcs, dsts=[_slot(T.s, k)] * per, alu_op=1))
+            else:
+                tr = [RemoteDMATransfer(
+                    dst_ids=[_dst(topo, c, core) for c in dsts], dma_engine_mask=0xFF,
+                    remote_sem=T.sem.got, srcs=srcs, dsts=[_slot(T.s, k)] * G, alu_op=1)]
+            g.remote_dma_fused(tr, local_sem=T.sem.sent)
+            g.wait_ge(T.sem.sent, 8)

@@ -1,7 +1,7 @@
 from concourse.bass import DstId, RemoteDMATransfer
 
 N = 16
-K = 4
+K = 8
 R = 2
 G = N // R
 W = 32 // K

@@ -5,7 +5,7 @@ K = 8
 R = 2
 G = N // R
 W = 32 // K
-SPLIT_FOLD = False
+E1 = 8 // K
 
 SCRATCH = {
     "d": ("dram", [K * 128, W], "bfloat16"),
@@ -32,56 +32,35 @@ def _dst(topo, dst, src):
     return DstId(rid=rid, pnc=pid)
 
 
-E1 = max(1, 8 // (K * R))
-E2 = max(1, 8 // G) if SPLIT_FOLD else 8
-
-
 def rank_program(g, core, T, topo):
     rank = T.rank_of(core)
     if rank is not None:
         g.sync.dma_start(T.d[:], T.x[:]).then_inc(T.sem.loaded, 16)
         g.wait_ge(T.sem.loaded, 16)
+        mine = rank // G
+        order = [q for q in range(R) if q != mine] + [mine]
         tr = []
-        if K * R <= 8:
-            for k in range(K):
-                for q in range(R):
-                    tr.append(RemoteDMATransfer(
-                        dst_ids=[_dst(topo, _reducer(T, k, q), core)], dma_engine_mask=_bits((k * R + q) * E1, E1),
-                        remote_sem=T.sem.arr, src=_slot(T.d, k), dst=_slot(T.land, rank)))
-            sent = 8
-        else:
-            e = 8 // K
-            for k in range(K):
-                tr.append(RemoteDMATransfer(
-                    dst_ids=[_dst(topo, _reducer(T, k, q), core) for q in range(R)], dma_engine_mask=_bits(k * e, e),
-                    remote_sem=T.sem.arr, srcs=[_slot(T.d, k)], dsts=[_slot(T.land, rank)] * R))
-            sent = 8
+        for k in range(K):
+            tr.append(RemoteDMATransfer(
+                dst_ids=[_dst(topo, _reducer(T, k, q), core) for q in order], dma_engine_mask=_bits(k * E1, E1),
+                remote_sem=T.sem.arr, srcs=[_slot(T.d, k)], dsts=[_slot(T.land, rank)] * R))
         g.remote_dma_fused(tr, local_sem=T.sem.sent)
         w0 = 2 * rank
-        g.sync.wait_ge(T.sem.got, K * E2)
+        g.sync.wait_ge(T.sem.got, K * 8)
         g.sync.dma_start(T.y[:], T.s[w0 // W::K, w0 % W:w0 % W + 2]).then_inc(T.sem.stored, 16)
         g.sync.wait_ge(T.sem.stored, 16)
-        g.wait_ge(T.sem.sent, sent)
+        g.wait_ge(T.sem.sent, 8)
         return
 
     for k in range(K):
         for q in range(R):
             if _reducer(T, k, q) != core:
                 continue
-            e1 = E1 if K * R <= 8 else 8 // K
-            g.wait_ge(T.sem.arr, N * e1)
+            g.wait_ge(T.sem.arr, N * E1)
             srcs = [_slot(T.land, i) for i in range(N)]
             dsts = [T.cores[q * G + j] for j in range(G)]
-            if SPLIT_FOLD:
-                per = max(1, G // 8)
-                tr = []
-                for j in range(0, G, per):
-                    tr.append(RemoteDMATransfer(
-                        dst_ids=[_dst(topo, c, core) for c in dsts[j:j + per]], dma_engine_mask=_bits((j // per) * E2, E2),
-                        remote_sem=T.sem.got, srcs=srcs, dsts=[_slot(T.s, k)] * per, alu_op=1))
-            else:
-                tr = [RemoteDMATransfer(
-                    dst_ids=[_dst(topo, c, core) for c in dsts], dma_engine_mask=0xFF,
-                    remote_sem=T.sem.got, srcs=srcs, dsts=[_slot(T.s, k)] * G, alu_op=1)]
-            g.remote_dma_fused(tr, local_sem=T.sem.sent)
+            dsts = [c for c in dsts if c != core - 1] + [c for c in dsts if c == core - 1]
+            g.remote_dma_fused([RemoteDMATransfer(
+                dst_ids=[_dst(topo, c, core) for c in dsts], dma_engine_mask=0xFF,
+                remote_sem=T.sem.got, srcs=srcs, dsts=[_slot(T.s, k)] * G, alu_op=1)], local_sem=T.sem.sent)
             g.wait_ge(T.sem.sent, 8)

from concourse.bass import DstId, RemoteDMATransfer

N = 16
K = 8
R = 2
G = N // R
W = 32 // K
E1 = 8 // K

SCRATCH = {
    "d": ("dram", [K * 128, W], "bfloat16"),
    "land": ("dram", [N * 128, W], "bfloat16"),
    "s": ("dram", [K * 128, W], "bfloat16"),
}
SEMAPHORES = ["loaded", "arr", "got", "sent", "stored"]


def _bits(first, n):
    return ((1 << n) - 1) << first


def _slot(t, i):
    return t[i * 128:(i + 1) * 128, :]


def _reducer(T, k, q):
    return T.cores[q * G + k * (G // K)] + 1


def _dst(topo, dst, src):
    rid, pid = topo.addr(dst, src)
    return DstId(rid=rid, pnc=pid)


def rank_program(g, core, T, topo):
    rank = T.rank_of(core)
    if rank is not None:
        g.sync.dma_start(T.d[:], T.x[:]).then_inc(T.sem.loaded, 16)
        g.wait_ge(T.sem.loaded, 16)
        mine = rank // G
        order = [q for q in range(R) if q != mine] + [mine]
        tr = []
        for k in range(K):
            tr.append(RemoteDMATransfer(
                dst_ids=[_dst(topo, _reducer(T, k, q), core) for q in order], dma_engine_mask=_bits(k * E1, E1),
                remote_sem=T.sem.arr, srcs=[_slot(T.d, k)], dsts=[_slot(T.land, rank)] * R))
        g.remote_dma_fused(tr, local_sem=T.sem.sent)
        w0 = 2 * rank
        g.sync.wait_ge(T.sem.got, K * 8)
        g.sync.dma_start(T.y[:], T.s[w0 // W::K, w0 % W:w0 % W + 2]).then_inc(T.sem.stored, 16)
        g.sync.wait_ge(T.sem.stored, 16)
        g.wait_ge(T.sem.sent, 8)
        return

    for k in range(K):
        for q in range(R):
            if _reducer(T, k, q) != core:
                continue
            g.wait_ge(T.sem.arr, N * E1)
            srcs = [_slot(T.land, i) for i in range(N)]
            dsts = [T.cores[q * G + j] for j in range(G)]
            dsts = [c for c in dsts if c != core - 1] + [c for c in dsts if c == core - 1]
            g.remote_dma_fused([RemoteDMATransfer(
                dst_ids=[_dst(topo, c, core) for c in dsts], dma_engine_mask=0xFF,
                remote_sem=T.sem.got, srcs=srcs, dsts=[_slot(T.s, k)] * G, alu_op=1)], local_sem=T.sem.sent)
            g.wait_ge(T.sem.sent, 8)
